import numpy as np
import ml_dtypes


def mxq(x, axis, fmt="e4m3"):
    dtype, down = {"e4m3": (ml_dtypes.float8_e4m3fn, 7), "e5m2": (ml_dtypes.float8_e5m2, 14)}[fmt]
    v = np.moveaxis(np.asarray(x, np.float32).astype(ml_dtypes.bfloat16).astype(np.float64), axis, -1)
    blocks = v.reshape(v.shape[:-1] + (-1, 32))
    amax = np.abs(blocks).max(-1, keepdims=True)
    byte = np.maximum(np.where(amax > 0, np.frexp(amax)[1] - 1 + 127, 0) - down, 1)
    scale = np.exp2(byte - 127.0)
    codes = (blocks / scale).astype(np.float32).astype(dtype).astype(np.float64)
    return np.moveaxis((codes * scale).reshape(v.shape), -1, axis)


WIDE = False


def mx_kscale(k, group=512):
    if not WIDE:
        return np.ones(k)
    levels = np.array([10, -10, 5, -5, 0])
    if group != 512:
        return np.exp2(np.random.permutation(np.resize(levels, k // group))).repeat(group)
    if k % 512:
        return np.exp2(np.random.permutation(np.resize(levels, k // 32))).repeat(32)
    a = np.empty((k // 512, 16))
    for p in range(k // 512):
        a[p, :8] = np.random.permutation(np.resize(levels, 8))
        for g in range(8):
            far = levels[np.abs(levels - a[p, g]) >= 10]
            a[p, g + 8] = far[np.random.randint(len(far))]
    return np.exp2(a.ravel()).repeat(32)


def f64(x):
    return np.asarray(x).astype(np.float64)


E2M1 = np.array([0.0, 0.5, 1.0, 1.5, 2.0, 3.0, 4.0, 6.0, -0.0, -0.5, -1.0, -1.5, -2.0, -3.0, -4.0, -6.0])


def pack_group(w):
    k, n = w.shape
    w = f64(np.asarray(w, np.float32).astype(ml_dtypes.bfloat16)).reshape(k // 32, 32, n)
    amax = np.abs(w).max(1)
    mant, ex = np.frexp(amax / 6.0)
    byte = np.clip(np.where(amax > 0, np.where(mant > 0.5, ex, ex - 1) + 127, 1), 1, 254)
    scaled = (w * np.exp2(127.0 - byte)[:, None, :]).reshape(k, n).astype(np.float32)
    c = np.ascontiguousarray(scaled.reshape(k // 4, 4, n).transpose(0, 2, 1)).astype(ml_dtypes.float4_e2m1fn).view(np.uint8) & 0xF
    return np.ascontiguousarray((c[..., 0::2] | (c[..., 1::2] << 4)).reshape(k // 4, 2 * n)), byte.astype(np.uint8)


def unpack_group(words, scales):
    p, n = words.shape[0], scales.shape[1]
    words = np.ascontiguousarray(words).reshape(p, n, 2)
    nib = np.empty((p, n, 4), np.uint8)
    nib[..., 0::2] = words & 0xF
    nib[..., 1::2] = words >> 4
    return E2M1[nib].transpose(0, 2, 1).reshape(4 * p, n) * np.repeat(np.exp2(scales.astype(np.float64) - 127.0), 32, axis=0)


G, D, M, O, N = 2, 256, 256, 256, 512


def setup_inputs():
    n = np.random.standard_normal
    s_d = mx_kscale(D, 0)
    s_o = mx_kscale(O, 0)
    w1_ = [pack_group(w) for w in n((G, D, M)) / np.sqrt(D) / s_d[:, None]]
    w2_ = [pack_group(w) for w in n((G, D, M)) / np.sqrt(D) / s_d[:, None]]
    wo_ = [pack_group(w) for w in n((G, O, M)) / np.sqrt(O) / s_o[:, None]]
    return {
        "x": (n((G, D, N)) * s_d[:, None]).astype(np.float32),
        "w1_words": np.stack([w[0] for w in w1_]),
        "w1_scales": np.stack([w[1] for w in w1_]),
        "w2_words": np.stack([w[0] for w in w2_]),
        "w2_scales": np.stack([w[1] for w in w2_]),
        "wo_words": np.stack([w[0] for w in wo_]),
        "wo_scales": np.stack([w[1] for w in wo_]),
        "dy": (n((G, O, N)) * s_o[:, None]).astype(np.float32),
        "old": (0.3 * n((G, M, N))).astype(np.float32),
    }


def reference(x, w1_words, w1_scales, w2_words, w2_scales, wo_words, wo_scales, dy, old):
    w1 = np.stack([unpack_group(w1_words[g], w1_scales[g]) for g in range(G)])
    xq = mxq(f64(x), 1, "e4m3")
    z1 = w1.transpose(0, 2, 1) @ xq
    w2 = np.stack([unpack_group(w2_words[g], w2_scales[g]) for g in range(G)])
    z2 = w2.transpose(0, 2, 1) @ xq
    pr = z1 * z2
    mu = np.mean(pr, axis=-1, keepdims=True)
    ms = np.sqrt(np.mean(np.square(z1), axis=-1, keepdims=True) + 0.1)
    wo = np.stack([unpack_group(wo_words[g], wo_scales[g]) for g in range(G)])
    dyq = mxq(f64(dy), 1, "e4m3")
    c0 = wo.transpose(0, 2, 1) @ dyq
    dms = np.sum(c0 * (pr - mu) / np.square(ms) * (-1.0), axis=-1, keepdims=True)
    dmu = np.sum(c0 / ms * (-1.0), axis=-1, keepdims=True)
    dpr = c0 / ms + dmu / 512.0
    dz1 = dms * 0.5 / np.sqrt(np.mean(np.square(z1), axis=-1, keepdims=True) + 0.1) / 512.0 * z1 * 2.0 + dpr * z2
    y = dz1 + f64(old)
    return y

@@ -1,0 +1,199 @@
+from contextlib import ExitStack
+
+import concourse.mybir as mybir
+
+G, D, M, N = 2, 256, 256, 512
+P = 128
+ROWS = 64
+PACK = 4
+RUN = 4
+EPS = 0.1
+
+F32 = mybir.dt.float32
+BF16 = mybir.dt.bfloat16
+I32 = mybir.dt.int32
+U32 = mybir.dt.uint32
+U8 = mybir.dt.uint8
+FP8X4 = mybir.dt.float8_e4m3fn_x4
+FP4X4 = mybir.dt.float4_e2m1fn_x4
+ALU = mybir.AluOpType
+ACT = mybir.ActivationFunctionType
+
+FLOPS = 3 * 2 * G * D * M * N
+
+SPLIT = 320
+
+
+def tile_rows_browcorr_kernel(tc, x, w1_words, w1_scales, w2_words, w2_scales, wo_words, wo_scales, dy, old, out):
+    nc = tc.nc
+    with ExitStack() as ctx:
+        sb = ctx.enter_context(tc.tile_pool(name="sb", bufs=1))
+        ps = ctx.enter_context(tc.psum_pool(name="ps", bufs=1))
+        ctx.enter_context(tc.manual_schedule())
+
+        dy_raw = sb.tile([P, PACK, N], F32, name="dy_raw")
+        x_raw = sb.tile([P, PACK, N], F32, name="x_raw")
+        old_sb = sb.tile([P, 4, N], F32, name="old_sb")
+        dy_bf = sb.tile([P, N * PACK], BF16, name="dy_bf", align_bytes=64)
+        x_bf = sb.tile([P, N * PACK], BF16, name="x_bf", align_bytes=64)
+        dy_codes = sb.tile([P, N], U32, name="dy_codes", align_bytes=64)
+        x_codes = sb.tile([P, N], U32, name="x_codes", align_bytes=64)
+        dy_plane = sb.tile([P, N], U8, name="dy_plane", align_bytes=64)
+        x_plane = sb.tile([P, N], U8, name="x_plane", align_bytes=64)
+        words = {k: sb.tile([P, 2 * M], U8, name=k + "_words_sb", align_bytes=64) for k in ("wo", "w2", "w1")}
+        plane = {k: sb.tile([P, M], U8, name=k + "_plane", align_bytes=64) for k in ("wo", "w2", "w1")}
+        rc = [sb.tile([P, N], F32, name="rc%d" % t) for t in range(4)]
+        u = [sb.tile([P, N], F32, name="u%d" % t) for t in range(4)]
+        part = [sb.tile([P, N], F32, name="part%d" % t) for t in range(4)]
+        res = [sb.tile([P, N], F32, name="res%d" % t) for t in range(4)]
+        sq = [sb.tile([P, N], BF16, name="sq%d" % t) for t in range(4)]
+        prod = [sb.tile([P, N], BF16, name="prod%d" % t) for t in range(4)]
+        rc_sum = sb.tile([P, 4], F32, name="rc_sum")
+        rc_mean = sb.tile([P, 4], F32, name="rc_mean")
+        sumsq = sb.tile([P, 4], F32, name="sumsq")
+        rinv = sb.tile([P, 4], F32, name="rinv")
+        r2 = sb.tile([P, 4], F32, name="r2")
+        r2n = sb.tile([P, 4], F32, name="r2n")
+        coef = sb.tile([P, 4], F32, name="coef")
+        z1_bank = [ps.tile([P, N], F32, name="z1_bank%d" % t) for t in range(4)]
+        z2_bank = [ps.tile([P, N], F32, name="z2_bank%d" % g) for g in range(G)]
+        c_bank = [ps.tile([P, N], F32, name="c_bank%d" % g) for g in range(G)]
+
+        def load_rows(dst, src):
+            nc.sync.dma_start(out=dst[:], in_=src.rearrange("g (p j) n -> (g p) j n", j=PACK))
+
+        def load_words(k, src):
+            nc.sync.dma_start(out=words[k][:].bitcast(I32), in_=src.rearrange("g p b -> (g p) b").bitcast(I32))
+
+        def load_scales(queue, k, src):
+            rows = src.rearrange("g f m -> (g f) m").bitcast(I32)
+            for q in range(4):
+                queue.dma_start(out=plane[k][32 * q : 32 * q + 4, :].bitcast(I32), in_=rows[4 * q : 4 * q + 4, :])
+
+        def views(dst, raw, c0, c1):
+            o = dst[:, PACK * c0 : PACK * c1].rearrange("p (c i j) -> p c j i", i=RUN, j=PACK)
+            i = raw[:, :, c0:c1].rearrange("p j (c i) -> p c j i", i=RUN)
+            return o, i
+
+        def cast_v(dst, raw, c0, c1):
+            o, i = views(dst, raw, c0, c1)
+            nc.vector.tensor_copy(out=o, in_=i)
+
+        def cast_s(dst, raw, c0, c1):
+            o, i = views(dst, raw, c0, c1)
+            nc.scalar.activation(out=o, in_=i, func=ACT.Copy)
+
+        def quant(codes, pl, src, c0, c1):
+            nc.vector.quantize_mx(out=codes[:, c0:c1].bitcast(FP8X4), scales=pl[:, c0:c1], in_=src[:, PACK * c0 : PACK * c1])
+
+        def product(bank, k, codes, pl, t):
+            g, h = t % 2, t // 2
+            rows = slice(ROWS * g, ROWS * g + ROWS)
+            nc.tensor.matmul_mx(
+                out=bank[:],
+                lhsT=words[k][rows, 2 * P * h : 2 * P * (h + 1)].bitcast(FP4X4),
+                lhsT_scale=plane[k][rows, P * h : P * (h + 1)],
+                rhs=codes[rows, :].bitcast(FP8X4),
+                rhs_scale=pl[rows, :],
+                start=True,
+                stop=True,
+            )
+
+        def col(tile, t):
+            return tile[:, t : t + 1]
+
+        def square(t):
+            nc.scalar.activation(out=sq[t][:], in_=z1_bank[t][:], func=ACT.Square, accum_out=col(sumsq, t))
+
+        def root(t):
+            nc.scalar.activation(out=col(rinv, t), in_=col(sumsq, t), func=ACT.Abs_reciprocal_sqrt, scale=1.0 / N, bias=EPS)
+
+        def root_sq(t0, t1):
+            nc.scalar.activation(out=r2[:, t0:t1], in_=rinv[:, t0:t1], func=ACT.Square)
+
+        def neg_scale(t0, t1):
+            nc.scalar.activation(out=r2n[:, t0:t1], in_=r2[:, t0:t1], func=ACT.Copy, scale=-1.0 / N)
+
+        def c_copy(t):
+            nc.scalar.activation(out=rc[t][:], in_=c_bank[t % 2][:], func=ACT.Identity, scale=col(rinv, t), accum_out=col(rc_sum, t))
+
+        def mean(t):
+            nc.scalar.activation(out=col(rc_mean, t), in_=col(rc_sum, t), func=ACT.Copy, scale=1.0 / N)
+
+        def centre(t):
+            nc.vector.scalar_tensor_tensor(out=u[t][:], in0=rc[t][:], scalar=col(rc_mean, t), in1=z2_bank[t % 2][:], op0=ALU.subtract, op1=ALU.mult)
+
+        def corr(t):
+            nc.vector.scalar_tensor_tensor(out=prod[t][:], in0=u[t][:], scalar=col(r2n, t), in1=z1_bank[t][:], op0=ALU.mult, op1=ALU.mult, accum_out=col(coef, t))
+
+        def add_old(t):
+            g, h = t % 2, t // 2
+            nc.gpsimd.tensor_tensor(out=part[t][:], in0=old_sb[:, 2 * g + h, :], in1=u[t][:], op=ALU.add)
+
+        def finish(t):
+            g, h = t % 2, t // 2
+            nc.vector.scalar_tensor_tensor(out=res[t][:], in0=z1_bank[t][:], scalar=col(coef, t), in1=part[t][:], op0=ALU.mult, op1=ALU.add)
+            nc.sync.dma_start(out=out[g, P * h : P * (h + 1), :], in_=res[t][:])
+
+        for k in ("w1", "wo", "w2"):
+            nc.vector.memset(plane[k][:].bitcast(I32), 0)
+        load_rows(x_raw, x)
+        load_scales(nc.scalar, "w1", w1_scales)
+        load_words("w1", w1_words)
+        load_rows(dy_raw, dy)
+        load_words("wo", wo_words)
+        load_words("w2", w2_words)
+        load_scales(nc.sync, "wo", wo_scales)
+        load_scales(nc.sync, "w2", w2_scales)
+        nc.sync.dma_start(out=old_sb[:], in_=old.rearrange("g (h p) n -> p (g h) n", p=P))
+
+        def quantise(codes, pl, bf, raw):
+            cast_v(bf, raw, 0, 256)
+            cast_s(bf, raw, SPLIT, N)
+            cast_v(bf, raw, 256, SPLIT)
+            quant(codes, pl, bf, 0, 256)
+            quant(codes, pl, bf, 256, N)
+
+        quantise(x_codes, x_plane, x_bf, x_raw)
+        for t in range(4):
+            product(z1_bank[t], "w1", x_codes, x_plane, t)
+        quantise(dy_codes, dy_plane, dy_bf, dy_raw)
+
+        def stats(a, b):
+            square(a)
+            square(b)
+            root(a)
+            root(b)
+            c_copy(a)
+            root_sq(a, a + 2)
+            mean(a)
+            c_copy(b)
+            neg_scale(a, a + 2)
+            mean(b)
+
+        for t in (0, 1):
+            product(z2_bank[t], "w2", x_codes, x_plane, t)
+        for t in (0, 1):
+            product(c_bank[t], "wo", dy_codes, dy_plane, t)
+        stats(0, 1)
+        centre(0)
+        centre(1)
+        for t in (2, 3):
+            product(c_bank[t % 2], "wo", dy_codes, dy_plane, t)
+        for t in (2, 3):
+            product(z2_bank[t % 2], "w2", x_codes, x_plane, t)
+        stats(2, 3)
+        add_old(0)
+        add_old(1)
+        corr(0)
+        corr(1)
+        finish(0)
+        centre(2)
+        add_old(2)
+        finish(1)
+        centre(3)
+        add_old(3)
+        corr(2)
+        corr(3)
+        finish(2)
+        finish(3)

@@ -21,7 +21,7 @@ ACT = mybir.ActivationFunctionType
 
 FLOPS = 3 * 2 * G * D * M * N
 
-SPLIT = 320
+SPLIT = 352
 
 
 def tile_rows_browcorr_kernel(tc, x, w1_words, w1_scales, w2_words, w2_scales, wo_words, wo_scales, dy, old, out):
@@ -33,7 +33,7 @@ def tile_rows_browcorr_kernel(tc, x, w1_words, w1_scales, w2_words, w2_scales, w
 
         dy_raw = sb.tile([P, PACK, N], F32, name="dy_raw")
         x_raw = sb.tile([P, PACK, N], F32, name="x_raw")
-        old_sb = sb.tile([P, 4, N], F32, name="old_sb")
+        old_sb = [sb.tile([P, G, N], F32, name="old_sb%d" % h) for h in range(2)]
         dy_bf = sb.tile([P, N * PACK], BF16, name="dy_bf", align_bytes=64)
         x_bf = sb.tile([P, N * PACK], BF16, name="x_bf", align_bytes=64)
         dy_codes = sb.tile([P, N], U32, name="dy_codes", align_bytes=64)
@@ -65,9 +65,9 @@ def tile_rows_browcorr_kernel(tc, x, w1_words, w1_scales, w2_words, w2_scales, w
         def load_words(k, src):
             nc.sync.dma_start(out=words[k][:].bitcast(I32), in_=src.rearrange("g p b -> (g p) b").bitcast(I32))
 
-        def load_scales(queue, k, src):
+        def load_scales(queue, k, src, quadrants=range(4)):
             rows = src.rearrange("g f m -> (g f) m").bitcast(I32)
-            for q in range(4):
+            for q in quadrants:
                 queue.dma_start(out=plane[k][32 * q : 32 * q + 4, :].bitcast(I32), in_=rows[4 * q : 4 * q + 4, :])
 
         def views(dst, raw, c0, c1):
@@ -117,6 +117,9 @@ def tile_rows_browcorr_kernel(tc, x, w1_words, w1_scales, w2_words, w2_scales, w
         def c_copy(t):
             nc.scalar.activation(out=rc[t][:], in_=c_bank[t % 2][:], func=ACT.Identity, scale=col(rinv, t), accum_out=col(rc_sum, t))
 
+        def c_copy_v(t):
+            nc.vector.tensor_scalar(out=rc[t][:], in0=c_bank[t % 2][:], scalar1=col(rinv, t), scalar2=None, op0=ALU.mult, op1=ALU.add, accum_out=col(rc_sum, t))
+
         def mean(t):
             nc.scalar.activation(out=col(rc_mean, t), in_=col(rc_sum, t), func=ACT.Copy, scale=1.0 / N)
 
@@ -128,24 +131,27 @@ def tile_rows_browcorr_kernel(tc, x, w1_words, w1_scales, w2_words, w2_scales, w
 
         def add_old(t):
             g, h = t % 2, t // 2
-            nc.gpsimd.tensor_tensor(out=part[t][:], in0=old_sb[:, 2 * g + h, :], in1=u[t][:], op=ALU.add)
+            nc.gpsimd.tensor_tensor(out=part[t][:], in0=old_sb[h][:, g, :], in1=u[t][:], op=ALU.add)
 
         def finish(t):
             g, h = t % 2, t // 2
             nc.vector.scalar_tensor_tensor(out=res[t][:], in0=z1_bank[t][:], scalar=col(coef, t), in1=part[t][:], op0=ALU.mult, op1=ALU.add)
             nc.sync.dma_start(out=out[g, P * h : P * (h + 1), :], in_=res[t][:])
 
-        for k in ("w1", "wo", "w2"):
+        for k in ("w1", "w2", "wo"):
             nc.vector.memset(plane[k][:].bitcast(I32), 0)
         load_rows(x_raw, x)
-        load_scales(nc.scalar, "w1", w1_scales)
+        load_scales(nc.sync, "w1", w1_scales)
+        load_scales(nc.gpsimd, "w2", w2_scales, (2, 3))
         load_words("w1", w1_words)
+        load_scales(nc.sync, "w2", w2_scales, (0,))
         load_rows(dy_raw, dy)
-        load_words("wo", wo_words)
         load_words("w2", w2_words)
+        load_scales(nc.sync, "w2", w2_scales, (1,))
+        load_words("wo", wo_words)
         load_scales(nc.sync, "wo", wo_scales)
-        load_scales(nc.sync, "w2", w2_scales)
-        nc.sync.dma_start(out=old_sb[:], in_=old.rearrange("g (h p) n -> p (g h) n", p=P))
+        for h in range(2):
+            nc.sync.dma_start(out=old_sb[h][:], in_=old[:, P * h : P * (h + 1), :].rearrange("g p n -> p g n"))
 
         def quantise(codes, pl, bf, raw):
             cast_v(bf, raw, 0, 256)
@@ -155,7 +161,7 @@ def tile_rows_browcorr_kernel(tc, x, w1_words, w1_scales, w2_words, w2_scales, w
             quant(codes, pl, bf, 256, N)
 
         quantise(x_codes, x_plane, x_bf, x_raw)
-        for t in range(4):
+        for t in (0, 1):
             product(z1_bank[t], "w1", x_codes, x_plane, t)
         quantise(dy_codes, dy_plane, dy_bf, dy_raw)
 
@@ -163,24 +169,34 @@ def tile_rows_browcorr_kernel(tc, x, w1_words, w1_scales, w2_words, w2_scales, w
             square(a)
             square(b)
             root(a)
-            root(b)
             c_copy(a)
-            root_sq(a, a + 2)
+            root(b)
             mean(a)
             c_copy(b)
-            neg_scale(a, a + 2)
+            root_sq(a, a + 2)
             mean(b)
+            neg_scale(a, a + 2)
 
         for t in (0, 1):
             product(z2_bank[t], "w2", x_codes, x_plane, t)
         for t in (0, 1):
             product(c_bank[t], "wo", dy_codes, dy_plane, t)
-        stats(0, 1)
+        for t in (2, 3):
+            product(z1_bank[t], "w1", x_codes, x_plane, t)
+        square(0)
+        square(1)
+        root(0)
+        root(1)
+        c_copy(0)
+        c_copy_v(1)
+        root_sq(0, 2)
+        mean(0)
+        neg_scale(0, 2)
+        mean(1)
         centre(0)
         centre(1)
         for t in (2, 3):
             product(c_bank[t % 2], "wo", dy_codes, dy_plane, t)
-        for t in (2, 3):
             product(z2_bank[t % 2], "w2", x_codes, x_plane, t)
         stats(2, 3)
         add_old(0)

@@ -21,7 +21,9 @@ ACT = mybir.ActivationFunctionType
 
 FLOPS = 3 * 2 * G * D * M * N
 
-SPLIT = 352
+TILES = ((0, 0), (1, 0), (0, 1), (1, 1))
+X_SPLIT = 352
+DY_SPLIT = 416
 
 
 def tile_rows_browcorr_kernel(tc, x, w1_words, w1_scales, w2_words, w2_scales, wo_words, wo_scales, dy, old, out):
@@ -87,7 +89,7 @@ def tile_rows_browcorr_kernel(tc, x, w1_words, w1_scales, w2_words, w2_scales, w
             nc.vector.quantize_mx(out=codes[:, c0:c1].bitcast(FP8X4), scales=pl[:, c0:c1], in_=src[:, PACK * c0 : PACK * c1])
 
         def product(bank, k, codes, pl, t):
-            g, h = t % 2, t // 2
+            g, h = TILES[t]
             rows = slice(ROWS * g, ROWS * g + ROWS)
             nc.tensor.matmul_mx(
                 out=bank[:],
@@ -105,8 +107,8 @@ def tile_rows_browcorr_kernel(tc, x, w1_words, w1_scales, w2_words, w2_scales, w
         def square(t):
             nc.scalar.activation(out=sq[t][:], in_=z1_bank[t][:], func=ACT.Square, accum_out=col(sumsq, t))
 
-        def root(t):
-            nc.scalar.activation(out=col(rinv, t), in_=col(sumsq, t), func=ACT.Abs_reciprocal_sqrt, scale=1.0 / N, bias=EPS)
+        def root(t0, t1):
+            nc.scalar.activation(out=rinv[:, t0:t1], in_=sumsq[:, t0:t1], func=ACT.Abs_reciprocal_sqrt, scale=1.0 / N, bias=EPS)
 
         def root_sq(t0, t1):
             nc.scalar.activation(out=r2[:, t0:t1], in_=rinv[:, t0:t1], func=ACT.Square)
@@ -115,29 +117,32 @@ def tile_rows_browcorr_kernel(tc, x, w1_words, w1_scales, w2_words, w2_scales, w
             nc.scalar.activation(out=r2n[:, t0:t1], in_=r2[:, t0:t1], func=ACT.Copy, scale=-1.0 / N)
 
         def c_copy(t):
-            nc.scalar.activation(out=rc[t][:], in_=c_bank[t % 2][:], func=ACT.Identity, scale=col(rinv, t), accum_out=col(rc_sum, t))
+            nc.scalar.activation(out=rc[t][:], in_=c_bank[TILES[t][0]][:], func=ACT.Identity, scale=col(rinv, t), accum_out=col(rc_sum, t))
 
         def c_copy_v(t):
-            nc.vector.tensor_scalar(out=rc[t][:], in0=c_bank[t % 2][:], scalar1=col(rinv, t), scalar2=None, op0=ALU.mult, op1=ALU.add, accum_out=col(rc_sum, t))
+            nc.vector.tensor_scalar(out=rc[t][:], in0=c_bank[TILES[t][0]][:], scalar1=col(rinv, t), scalar2=None, op0=ALU.mult, op1=ALU.add, accum_out=col(rc_sum, t))
 
         def mean(t):
             nc.scalar.activation(out=col(rc_mean, t), in_=col(rc_sum, t), func=ACT.Copy, scale=1.0 / N)
 
         def centre(t):
-            nc.vector.scalar_tensor_tensor(out=u[t][:], in0=rc[t][:], scalar=col(rc_mean, t), in1=z2_bank[t % 2][:], op0=ALU.subtract, op1=ALU.mult)
+            nc.vector.scalar_tensor_tensor(out=u[t][:], in0=rc[t][:], scalar=col(rc_mean, t), in1=z2_bank[TILES[t][0]][:], op0=ALU.subtract, op1=ALU.mult)
 
         def corr(t):
             nc.vector.scalar_tensor_tensor(out=prod[t][:], in0=u[t][:], scalar=col(r2n, t), in1=z1_bank[t][:], op0=ALU.mult, op1=ALU.mult, accum_out=col(coef, t))
 
         def add_old(t):
-            g, h = t % 2, t // 2
+            g, h = TILES[t]
             nc.gpsimd.tensor_tensor(out=part[t][:], in0=old_sb[h][:, g, :], in1=u[t][:], op=ALU.add)
 
         def finish(t):
-            g, h = t % 2, t // 2
+            g, h = TILES[t]
             nc.vector.scalar_tensor_tensor(out=res[t][:], in0=z1_bank[t][:], scalar=col(coef, t), in1=part[t][:], op0=ALU.mult, op1=ALU.add)
             nc.sync.dma_start(out=out[g, P * h : P * (h + 1), :], in_=res[t][:])
 
+        warm = sb.tile([P, 2], F32, name="warm")
+        nc.vector.memset(warm[:, 0:1], 1.0)
+        nc.scalar.activation(out=warm[:, 1:2], in_=warm[:, 0:1], func=ACT.Abs_reciprocal_sqrt)
         for k in ("w1", "w2", "wo"):
             nc.vector.memset(plane[k][:].bitcast(I32), 0)
         load_rows(x_raw, x)
@@ -153,62 +158,56 @@ def tile_rows_browcorr_kernel(tc, x, w1_words, w1_scales, w2_words, w2_scales, w
         for h in range(2):
             nc.sync.dma_start(out=old_sb[h][:], in_=old[:, P * h : P * (h + 1), :].rearrange("g p n -> p g n"))
 
-        def quantise(codes, pl, bf, raw):
+        def quantise(codes, pl, bf, raw, split):
             cast_v(bf, raw, 0, 256)
-            cast_s(bf, raw, SPLIT, N)
-            cast_v(bf, raw, 256, SPLIT)
+            cast_s(bf, raw, split, N)
+            cast_v(bf, raw, 256, split)
             quant(codes, pl, bf, 0, 256)
             quant(codes, pl, bf, 256, N)
 
-        quantise(x_codes, x_plane, x_bf, x_raw)
-        for t in (0, 1):
+        quantise(x_codes, x_plane, x_bf, x_raw, X_SPLIT)
+        for t in (0, 1, 2):
             product(z1_bank[t], "w1", x_codes, x_plane, t)
-        quantise(dy_codes, dy_plane, dy_bf, dy_raw)
-
-        def stats(a, b):
-            square(a)
-            square(b)
-            root(a)
-            c_copy(a)
-            root(b)
-            mean(a)
-            c_copy(b)
-            root_sq(a, a + 2)
-            mean(b)
-            neg_scale(a, a + 2)
-
-        for t in (0, 1):
-            product(z2_bank[t], "w2", x_codes, x_plane, t)
+        product(z2_bank[0], "w2", x_codes, x_plane, 0)
+        square(0)
+        quantise(dy_codes, dy_plane, dy_bf, dy_raw, DY_SPLIT)
         for t in (0, 1):
             product(c_bank[t], "wo", dy_codes, dy_plane, t)
-        for t in (2, 3):
-            product(z1_bank[t], "w1", x_codes, x_plane, t)
-        square(0)
+        product(z2_bank[1], "w2", x_codes, x_plane, 1)
+        product(z1_bank[3], "w1", x_codes, x_plane, 3)
         square(1)
-        root(0)
-        root(1)
+        square(2)
+        root(0, 2)
+        root(2, 3)
         c_copy(0)
         c_copy_v(1)
-        root_sq(0, 2)
+        root_sq(0, 3)
         mean(0)
-        neg_scale(0, 2)
+        neg_scale(0, 3)
         mean(1)
         centre(0)
         centre(1)
         for t in (2, 3):
-            product(c_bank[t % 2], "wo", dy_codes, dy_plane, t)
-            product(z2_bank[t % 2], "w2", x_codes, x_plane, t)
-        stats(2, 3)
+            product(c_bank[TILES[t][0]], "wo", dy_codes, dy_plane, t)
+            product(z2_bank[TILES[t][0]], "w2", x_codes, x_plane, t)
+        square(3)
+        c_copy(2)
+        root(3, 4)
+        mean(2)
+        c_copy(3)
+        root_sq(3, 4)
+        mean(3)
+        neg_scale(3, 4)
         add_old(0)
         add_old(1)
         corr(0)
         corr(1)
-        finish(0)
         centre(2)
         add_old(2)
-        finish(1)
+        finish(0)
         centre(3)
         add_old(3)
+        finish(1)
         corr(2)
         corr(3)
         finish(2)

from contextlib import ExitStack

import concourse.mybir as mybir

G, D, M, N = 2, 256, 256, 512
P = 128
ROWS = 64
PACK = 4
RUN = 4
EPS = 0.1

F32 = mybir.dt.float32
BF16 = mybir.dt.bfloat16
I32 = mybir.dt.int32
U32 = mybir.dt.uint32
U8 = mybir.dt.uint8
FP8X4 = mybir.dt.float8_e4m3fn_x4
FP4X4 = mybir.dt.float4_e2m1fn_x4
ALU = mybir.AluOpType
ACT = mybir.ActivationFunctionType

FLOPS = 3 * 2 * G * D * M * N

TILES = ((0, 0), (1, 0), (0, 1), (1, 1))
X_SPLIT = 352
DY_SPLIT = 416


def tile_rows_browcorr_kernel(tc, x, w1_words, w1_scales, w2_words, w2_scales, wo_words, wo_scales, dy, old, out):
    nc = tc.nc
    with ExitStack() as ctx:
        sb = ctx.enter_context(tc.tile_pool(name="sb", bufs=1))
        ps = ctx.enter_context(tc.psum_pool(name="ps", bufs=1))
        ctx.enter_context(tc.manual_schedule())

        dy_raw = sb.tile([P, PACK, N], F32, name="dy_raw")
        x_raw = sb.tile([P, PACK, N], F32, name="x_raw")
        old_sb = [sb.tile([P, G, N], F32, name="old_sb%d" % h) for h in range(2)]
        dy_bf = sb.tile([P, N * PACK], BF16, name="dy_bf", align_bytes=64)
        x_bf = sb.tile([P, N * PACK], BF16, name="x_bf", align_bytes=64)
        dy_codes = sb.tile([P, N], U32, name="dy_codes", align_bytes=64)
        x_codes = sb.tile([P, N], U32, name="x_codes", align_bytes=64)
        dy_plane = sb.tile([P, N], U8, name="dy_plane", align_bytes=64)
        x_plane = sb.tile([P, N], U8, name="x_plane", align_bytes=64)
        words = {k: sb.tile([P, 2 * M], U8, name=k + "_words_sb", align_bytes=64) for k in ("wo", "w2", "w1")}
        plane = {k: sb.tile([P, M], U8, name=k + "_plane", align_bytes=64) for k in ("wo", "w2", "w1")}
        rc = [sb.tile([P, N], F32, name="rc%d" % t) for t in range(4)]
        u = [sb.tile([P, N], F32, name="u%d" % t) for t in range(4)]
        part = [sb.tile([P, N], F32, name="part%d" % t) for t in range(4)]
        res = [sb.tile([P, N], F32, name="res%d" % t) for t in range(4)]
        sq = [sb.tile([P, N], BF16, name="sq%d" % t) for t in range(4)]
        prod = [sb.tile([P, N], BF16, name="prod%d" % t) for t in range(4)]
        rc_sum = sb.tile([P, 4], F32, name="rc_sum")
        rc_mean = sb.tile([P, 4], F32, name="rc_mean")
        sumsq = sb.tile([P, 4], F32, name="sumsq")
        rinv = sb.tile([P, 4], F32, name="rinv")
        r2 = sb.tile([P, 4], F32, name="r2")
        r2n = sb.tile([P, 4], F32, name="r2n")
        coef = sb.tile([P, 4], F32, name="coef")
        z1_bank = [ps.tile([P, N], F32, name="z1_bank%d" % t) for t in range(4)]
        z2_bank = [ps.tile([P, N], F32, name="z2_bank%d" % g) for g in range(G)]
        c_bank = [ps.tile([P, N], F32, name="c_bank%d" % g) for g in range(G)]

        def load_rows(dst, src):
            nc.sync.dma_start(out=dst[:], in_=src.rearrange("g (p j) n -> (g p) j n", j=PACK))

        def load_words(k, src):
            nc.sync.dma_start(out=words[k][:].bitcast(I32), in_=src.rearrange("g p b -> (g p) b").bitcast(I32))

        def load_scales(queue, k, src, quadrants=range(4)):
            rows = src.rearrange("g f m -> (g f) m").bitcast(I32)
            for q in quadrants:
                queue.dma_start(out=plane[k][32 * q : 32 * q + 4, :].bitcast(I32), in_=rows[4 * q : 4 * q + 4, :])

        def views(dst, raw, c0, c1):
            o = dst[:, PACK * c0 : PACK * c1].rearrange("p (c i j) -> p c j i", i=RUN, j=PACK)
            i = raw[:, :, c0:c1].rearrange("p j (c i) -> p c j i", i=RUN)
            return o, i

        def cast_v(dst, raw, c0, c1):
            o, i = views(dst, raw, c0, c1)
            nc.vector.tensor_copy(out=o, in_=i)

        def cast_s(dst, raw, c0, c1):
            o, i = views(dst, raw, c0, c1)
            nc.scalar.activation(out=o, in_=i, func=ACT.Copy)

        def quant(codes, pl, src, c0, c1):
            nc.vector.quantize_mx(out=codes[:, c0:c1].bitcast(FP8X4), scales=pl[:, c0:c1], in_=src[:, PACK * c0 : PACK * c1])

        def product(bank, k, codes, pl, t):
            g, h = TILES[t]
            rows = slice(ROWS * g, ROWS * g + ROWS)
            nc.tensor.matmul_mx(
                out=bank[:],
                lhsT=words[k][rows, 2 * P * h : 2 * P * (h + 1)].bitcast(FP4X4),
                lhsT_scale=plane[k][rows, P * h : P * (h + 1)],
                rhs=codes[rows, :].bitcast(FP8X4),
                rhs_scale=pl[rows, :],
                start=True,
                stop=True,
            )

        def col(tile, t):
            return tile[:, t : t + 1]

        def square(t):
            nc.scalar.activation(out=sq[t][:], in_=z1_bank[t][:], func=ACT.Square, accum_out=col(sumsq, t))

        def root(t0, t1):
            nc.scalar.activation(out=rinv[:, t0:t1], in_=sumsq[:, t0:t1], func=ACT.Abs_reciprocal_sqrt, scale=1.0 / N, bias=EPS)

        def root_sq(t0, t1):
            nc.scalar.activation(out=r2[:, t0:t1], in_=rinv[:, t0:t1], func=ACT.Square)

        def neg_scale(t0, t1):
            nc.scalar.activation(out=r2n[:, t0:t1], in_=r2[:, t0:t1], func=ACT.Copy, scale=-1.0 / N)

        def c_copy(t):
            nc.scalar.activation(out=rc[t][:], in_=c_bank[TILES[t][0]][:], func=ACT.Identity, scale=col(rinv, t), accum_out=col(rc_sum, t))

        def c_copy_v(t):
            nc.vector.tensor_scalar(out=rc[t][:], in0=c_bank[TILES[t][0]][:], scalar1=col(rinv, t), scalar2=None, op0=ALU.mult, op1=ALU.add, accum_out=col(rc_sum, t))

        def mean(t):
            nc.scalar.activation(out=col(rc_mean, t), in_=col(rc_sum, t), func=ACT.Copy, scale=1.0 / N)

        def centre(t):
            nc.vector.scalar_tensor_tensor(out=u[t][:], in0=rc[t][:], scalar=col(rc_mean, t), in1=z2_bank[TILES[t][0]][:], op0=ALU.subtract, op1=ALU.mult)

        def corr(t):
            nc.vector.scalar_tensor_tensor(out=prod[t][:], in0=u[t][:], scalar=col(r2n, t), in1=z1_bank[t][:], op0=ALU.mult, op1=ALU.mult, accum_out=col(coef, t))

        def add_old(t):
            g, h = TILES[t]
            nc.gpsimd.tensor_tensor(out=part[t][:], in0=old_sb[h][:, g, :], in1=u[t][:], op=ALU.add)

        def finish(t):
            g, h = TILES[t]
            nc.vector.scalar_tensor_tensor(out=res[t][:], in0=z1_bank[t][:], scalar=col(coef, t), in1=part[t][:], op0=ALU.mult, op1=ALU.add)
            nc.sync.dma_start(out=out[g, P * h : P * (h + 1), :], in_=res[t][:])

        warm = sb.tile([P, 2], F32, name="warm")
        nc.vector.memset(warm[:, 0:1], 1.0)
        nc.scalar.activation(out=warm[:, 1:2], in_=warm[:, 0:1], func=ACT.Abs_reciprocal_sqrt)
        for k in ("w1", "w2", "wo"):
            nc.vector.memset(plane[k][:].bitcast(I32), 0)
        load_rows(x_raw, x)
        load_scales(nc.sync, "w1", w1_scales)
        load_scales(nc.gpsimd, "w2", w2_scales, (2, 3))
        load_words("w1", w1_words)
        load_scales(nc.sync, "w2", w2_scales, (0,))
        load_rows(dy_raw, dy)
        load_words("w2", w2_words)
        load_scales(nc.sync, "w2", w2_scales, (1,))
        load_words("wo", wo_words)
        load_scales(nc.sync, "wo", wo_scales)
        for h in range(2):
            nc.sync.dma_start(out=old_sb[h][:], in_=old[:, P * h : P * (h + 1), :].rearrange("g p n -> p g n"))

        def quantise(codes, pl, bf, raw, split):
            cast_v(bf, raw, 0, 256)
            cast_s(bf, raw, split, N)
            cast_v(bf, raw, 256, split)
            quant(codes, pl, bf, 0, 256)
            quant(codes, pl, bf, 256, N)

        quantise(x_codes, x_plane, x_bf, x_raw, X_SPLIT)
        for t in (0, 1, 2):
            product(z1_bank[t], "w1", x_codes, x_plane, t)
        product(z2_bank[0], "w2", x_codes, x_plane, 0)
        square(0)
        quantise(dy_codes, dy_plane, dy_bf, dy_raw, DY_SPLIT)
        for t in (0, 1):
            product(c_bank[t], "wo", dy_codes, dy_plane, t)
        product(z2_bank[1], "w2", x_codes, x_plane, 1)
        product(z1_bank[3], "w1", x_codes, x_plane, 3)
        square(1)
        square(2)
        root(0, 2)
        root(2, 3)
        c_copy(0)
        c_copy_v(1)
        root_sq(0, 3)
        mean(0)
        neg_scale(0, 3)
        mean(1)
        centre(0)
        centre(1)
        for t in (2, 3):
            product(c_bank[TILES[t][0]], "wo", dy_codes, dy_plane, t)
            product(z2_bank[TILES[t][0]], "w2", x_codes, x_plane, t)
        square(3)
        c_copy(2)
        root(3, 4)
        mean(2)
        c_copy(3)
        root_sq(3, 4)
        mean(3)
        neg_scale(3, 4)
        add_old(0)
        add_old(1)
        corr(0)
        corr(1)
        centre(2)
        add_old(2)
        finish(0)
        centre(3)
        add_old(3)
        finish(1)
        corr(2)
        corr(3)
        finish(2)
        finish(3)
